import numpy as np
import ml_dtypes


def mxq(x, axis, fmt="e4m3"):
    dtype, down = {"e4m3": (ml_dtypes.float8_e4m3fn, 7), "e5m2": (ml_dtypes.float8_e5m2, 14)}[fmt]
    v = np.moveaxis(np.asarray(x, np.float32).astype(ml_dtypes.bfloat16).astype(np.float64), axis, -1)
    blocks = v.reshape(v.shape[:-1] + (-1, 32))
    amax = np.abs(blocks).max(-1, keepdims=True)
    byte = np.maximum(np.where(amax > 0, np.frexp(amax)[1] - 1 + 127, 0) - down, 1)
    scale = np.exp2(byte - 127.0)
    codes = (blocks / scale).astype(np.float32).astype(dtype).astype(np.float64)
    return np.moveaxis((codes * scale).reshape(v.shape), -1, axis)


WIDE = False


def mx_kscale(k):
    if not WIDE:
        return np.ones(k)
    levels = np.array([30, -30])
    if k % 512:
        return np.exp2(np.random.permutation(np.resize(levels, k // 32))).repeat(32)
    a = np.empty((k // 512, 16))
    for p in range(k // 512):
        a[p, :8] = np.random.permutation(np.resize(levels, 8))
        for g in range(8):
            far = levels[np.abs(levels - a[p, g]) >= 10]
            a[p, g + 8] = far[np.random.randint(len(far))]
    return np.exp2(a.ravel()).repeat(32)


def f64(x):
    return np.asarray(x).astype(np.float64)


def striped(idx):
    return np.tile(np.asarray(idx).reshape(-1, 16).T, (8, 1)).astype(np.uint16)


def unstriped(offs):
    return offs[:16].T.reshape(-1).astype(np.int64)


E2M1 = np.array([0.0, 0.5, 1.0, 1.5, 2.0, 3.0, 4.0, 6.0, -0.0, -0.5, -1.0, -1.5, -2.0, -3.0, -4.0, -6.0])


def pack_weight(w, fmt):
    k, n = w.shape
    w = f64(np.asarray(w, np.float32).astype(ml_dtypes.bfloat16)).reshape(k // 32, 32, n)
    amax = np.abs(w).max(1)
    if fmt in ("e4m3", "e5m2"):
        byte = np.frexp(amax)[1] - 1 + 127 - (7 if fmt == "e4m3" else 14)
    else:
        mant, ex = np.frexp(amax / 6.0)
        byte = np.where(mant > 0.5, ex, ex - 1) + 127
    byte = np.clip(np.where(amax > 0, byte, 1), 1, 254)
    scaled = (w * np.exp2(127.0 - byte)[:, None, :]).reshape(k, n).astype(np.float32)
    by_word = np.ascontiguousarray(scaled.reshape(k // 512, 128, 4, n).transpose(0, 1, 3, 2))
    if fmt in ("e4m3", "e5m2"):
        words = by_word.astype(ml_dtypes.float8_e4m3fn if fmt == "e4m3" else ml_dtypes.float8_e5m2).view(np.uint8)
    else:
        c = by_word.astype(ml_dtypes.float4_e2m1fn).view(np.uint8) & 0xF
        words = (c[..., 0::2] | (c[..., 1::2] << 4)).reshape(k // 512, 128, 2 * n)
    return np.ascontiguousarray(words), np.ascontiguousarray(byte.astype(np.uint8).reshape(k // 512, 16, n))


def unpack_weight(words, scales, fmt):
    g, _, n = scales.shape
    words = np.ascontiguousarray(words).reshape(g, 128, n, -1)
    if fmt in ("e4m3", "e5m2"):
        vals = words.view(ml_dtypes.float8_e4m3fn if fmt == "e4m3" else ml_dtypes.float8_e5m2).astype(np.float64)
    else:
        nib = np.empty((g, 128, n, 4), np.uint8)
        nib[..., 0::2] = words & 0xF
        nib[..., 1::2] = words >> 4
        vals = E2M1[nib]
    vals = vals * np.repeat(np.exp2(scales.astype(np.float64) - 127.0), 8, axis=1)[..., None]
    return vals.transpose(0, 1, 3, 2).reshape(g * 512, n)


K, T, J, R, C, N, E = 512, 2048, 256, 512, 512, 256, 1024


def setup_inputs():
    n = np.random.standard_normal
    idx = np.random.permutation(T)[:J]
    idx2 = np.random.permutation(T)[:J]
    idx3 = np.random.permutation(C)[:J]
    idx4 = np.random.permutation(C)[:J]
    idx5 = np.random.permutation(E)[:J]
    fk = mx_kscale(K)
    fr = mx_kscale(R)
    xtp = pack_weight(n((K, T)) / fk[:, None], "e2m1")
    wp = pack_weight(n((K, R)) * 1 / np.sqrt(K) * fk[:, None] * fr, "e4m3")
    w2p = pack_weight(n((K, R)) * 1 / np.sqrt(K) * fk[:, None] * fr, "e5m2")
    wbp = pack_weight(n((R, N)) * 1 / np.sqrt(R) / fr[:, None], "e2m1")
    return {
        "xt_words": xtp[0],
        "xt_scales": xtp[1],
        "w_words": wp[0],
        "w_scales": wp[1],
        "w2_words": w2p[0],
        "w2_scales": w2p[1],
        "wb_words": wbp[0],
        "wb_scales": wbp[1],
        "tz": (n((N, E))).astype(np.float32),
        "offs": striped(idx),
        "offs2": striped(idx2),
        "offs3": striped(idx3),
        "offs4": striped(idx4),
        "offs5": striped(idx5),
    }


def reference(xt_words, xt_scales, w_words, w_scales, w2_words, w2_scales, wb_words, wb_scales, tz, offs, offs2, offs3, offs4, offs5):
    idx = unstriped(offs)
    idx2 = unstriped(offs2)
    idx3 = unstriped(offs3)
    idx4 = unstriped(offs4)
    idx5 = unstriped(offs5)
    xtu = unpack_weight(xt_words, xt_scales, "e2m1")
    wu = unpack_weight(w_words, w_scales, "e4m3")
    w2u = unpack_weight(w2_words, w2_scales, "e5m2")
    wbu = unpack_weight(wb_words, wb_scales, "e2m1")
    xtidxg = xtu[:, idx]
    a = wu.T @ xtidxg
    xtidx2g = xtu[:, idx2]
    b = w2u.T @ xtidx2g
    pw = np.zeros((R, C))
    pw[:, idx3] = a
    hid = np.abs(pw[:, idx4] - b)
    hidq = mxq(hid, 0, "e5m2")
    p = wbu.T @ hidq
    y = p + f64(tz)[:, idx5]
    return y

@@ -1,0 +1,192 @@
+from contextlib import ExitStack
+
+import concourse.mybir as mybir
+
+K, T, J, R, C, N, E = 512, 2048, 256, 512, 512, 256, 1024
+FLOPS = 2 * (2 * K * R * J + R * N * J)
+
+F32 = mybir.dt.float32
+BF16 = mybir.dt.bfloat16
+I32 = mybir.dt.int32
+U32 = mybir.dt.uint32
+U16 = mybir.dt.uint16
+U8 = mybir.dt.uint8
+E4M3 = mybir.dt.float8_e4m3fn_x4
+E5M2 = mybir.dt.float8_e5m2_x4
+E2M1 = mybir.dt.float4_e2m1fn_x4
+ALU = mybir.AluOpType
+ACT = mybir.ActivationFunctionType
+
+P = 128
+PACK = 4
+QUAD = 32
+HALVES = 2
+JH = J // HALVES
+
+
+def load_rows(queue, plane, scales, q):
+    rows = scales[0].bitcast(I32)
+    queue.dma_start(out=plane[QUAD * q : QUAD * q + 4, :].bitcast(I32), in_=rows[4 * q : 4 * q + 4, :])
+
+
+def load_rows_repeated(queue, plane, scales, q):
+    rows = scales[0].bitcast(I32)
+    queue.dma_start(
+        out=plane[QUAD * q : QUAD * (q + 1), :].bitcast(I32),
+        in_=rows[4 * q : 4 * q + 4, :].partition_broadcast(QUAD // 4),
+    )
+
+
+def tile_list_ahead_board_one_tabled_kernel(
+    tc, xt_words, xt_scales, w_words, w_scales, w2_words, w2_scales, wb_words, wb_scales, tz,
+    offs, offs2, offs3, offs4, offs5, out,
+):
+    nc = tc.nc
+    with ExitStack() as ctx:
+        lists = ctx.enter_context(tc.tile_pool(name="lists", bufs=1))
+        sb = ctx.enter_context(tc.tile_pool(name="sb", bufs=1))
+        ps = ctx.enter_context(tc.psum_pool(name="ps", bufs=1))
+
+        l1 = lists.tile([P, J // 16], U16, name="l1")
+        l2 = lists.tile([P, J // 16], U16, name="l2")
+        l3 = lists.tile([P, J // 16], U16, name="l3")
+        l4 = lists.tile([P, J // 16], U16, name="l4")
+        l5 = lists.tile([P, J // 16], U16, name="l5")
+
+        xw = sb.tile([P, T], U16, name="xw", align_bytes=64)
+        xs = sb.tile([P, T], U8, name="xs", align_bytes=64)
+        w_raw = sb.tile([P, R], U32, name="w_raw", align_bytes=64)
+        ws_raw = sb.tile([P, R], U8, name="ws_raw", align_bytes=64)
+        w2_raw = sb.tile([P, R], U32, name="w2_raw", align_bytes=64)
+        w2s_raw = sb.tile([P, R], U8, name="w2s_raw", align_bytes=64)
+        wb = sb.tile([P, 2 * N], U8, name="wb", align_bytes=64)
+        wbs = sb.tile([P, N], U8, name="wbs", align_bytes=64)
+        tzt = [sb.tile([P, E], F32, name=f"tz{u}", align_bytes=64) for u in range(N // P)]
+        board = [sb.tile([P, C], F32, name=f"board{t}", align_bytes=64) for t in range(PACK)]
+
+        nc.vector.memset(xs[:].bitcast(I32), 0)
+        for t in range(PACK):
+            nc.vector.memset(board[t][:], 0.0)
+        nc.sync.dma_start(l1[:], offs)
+        load_rows_repeated(nc.sync, ws_raw, w_scales, 0)
+        load_rows_repeated(nc.sync, ws_raw, w_scales, 1)
+        load_rows_repeated(nc.sync, ws_raw, w_scales, 2)
+        load_rows_repeated(nc.sync, ws_raw, w_scales, 3)
+        nc.sync.dma_start(out=xw[:].bitcast(I32), in_=xt_words[0].bitcast(I32))
+        load_rows(nc.sync, xs, xt_scales, 0)
+        load_rows(nc.sync, xs, xt_scales, 1)
+        load_rows(nc.sync, xs, xt_scales, 2)
+        load_rows(nc.sync, xs, xt_scales, 3)
+        nc.sync.dma_start(out=w_raw[:].bitcast(I32), in_=w_words[0].rearrange("p n t -> p (n t)").bitcast(I32))
+        nc.sync.dma_start(l2[:], offs2)
+        nc.sync.dma_start(out=w2_raw[:].bitcast(I32), in_=w2_words[0].rearrange("p n t -> p (n t)").bitcast(I32))
+        nc.sync.dma_start(l3[:], offs3)
+        load_rows_repeated(nc.sync, w2s_raw, w2_scales, 0)
+        load_rows_repeated(nc.sync, w2s_raw, w2_scales, 1)
+        load_rows_repeated(nc.sync, w2s_raw, w2_scales, 2)
+        load_rows_repeated(nc.sync, w2s_raw, w2_scales, 3)
+        nc.sync.dma_start(l4[:], offs4)
+        nc.sync.dma_start(out=wb[:].bitcast(I32), in_=wb_words[0].bitcast(I32))
+        load_rows_repeated(nc.sync, wbs, wb_scales, 0)
+        load_rows_repeated(nc.sync, wbs, wb_scales, 1)
+        load_rows_repeated(nc.sync, wbs, wb_scales, 2)
+        load_rows_repeated(nc.sync, wbs, wb_scales, 3)
+        nc.sync.dma_start(l5[:], offs5)
+        nc.sync.dma_start(out=tzt[0][:], in_=tz[0:P, :])
+        nc.sync.dma_start(out=tzt[1][:], in_=tz[P : 2 * P, :])
+
+        def dealt(tile):
+            return tile[:].rearrange("p (t m) -> p m t", t=PACK)
+
+        def as_given(tile):
+            return tile[:].rearrange("p (m t) -> p m t", t=PACK)
+
+        x1s = sb.tile([P, J], U8, name="x1s", align_bytes=64)
+        x1w = sb.tile([P, J], U16, name="x1w", align_bytes=64)
+        x2s = sb.tile([P, J], U8, name="x2s", align_bytes=64)
+        x2w = sb.tile([P, J], U16, name="x2w", align_bytes=64)
+        w = sb.tile([P, R], U32, name="w", align_bytes=64)
+        ws = sb.tile([P, R], U8, name="ws", align_bytes=64)
+        w2 = sb.tile([P, R], U32, name="w2", align_bytes=64)
+        w2s = sb.tile([P, R], U8, name="w2s", align_bytes=64)
+
+        nc.vector.tensor_copy(x1s[:], xs[:].indirect(l1[:]))
+        nc.vector.tensor_copy(x1w[:], xw[:].indirect(l1[:]))
+        nc.scalar.copy(dealt(w), as_given(w_raw))
+        nc.vector.tensor_copy(dealt(ws), as_given(ws_raw))
+        nc.scalar.copy(dealt(w2), as_given(w2_raw))
+
+        a_ps = [ps.tile([P, J], F32, name=f"a_ps{t}") for t in range(PACK)]
+        for t in range(PACK):
+            cols = slice(t * P, (t + 1) * P)
+            nc.tensor.matmul_mx(
+                out=a_ps[t][:], lhsT=w[:, cols].bitcast(E4M3), lhsT_scale=ws[:, cols],
+                rhs=x1w[:].bitcast(E2M1), rhs_scale=x1s[:], start=True, stop=True,
+            )
+
+        nc.vector.tensor_copy(x2s[:], xs[:].indirect(l2[:]))
+        nc.vector.tensor_copy(x2w[:], xw[:].indirect(l2[:]))
+        nc.vector.tensor_copy(dealt(w2s), as_given(w2s_raw))
+        b_ps = [ps.tile([P, PACK, JH], F32, name=f"b_ps{h}") for h in range(HALVES)]
+        for h in range(HALVES):
+            js = slice(h * JH, (h + 1) * JH)
+            for t in range(PACK):
+                cols = slice(t * P, (t + 1) * P)
+                nc.tensor.matmul_mx(
+                    out=b_ps[h][:, t, :], lhsT=w2[:, cols].bitcast(E5M2), lhsT_scale=w2s[:, cols],
+                    rhs=x2w[:, js].bitcast(E2M1), rhs_scale=x2s[:, js], start=True, stop=True,
+                )
+
+        a_sb = [sb.tile([P, J], F32, name=f"a_sb{t}", align_bytes=64) for t in range(PACK)]
+        nc.scalar.copy(a_sb[0][:], a_ps[0][:])
+        nc.scalar.copy(a_sb[1][:], a_ps[1][:])
+        nc.vector.tensor_copy(board[0][:].indirect(l3[:]), a_sb[0][:])
+        nc.scalar.activation(board[1][:].indirect(l3[:]), a_sb[1][:], ACT.Copy)
+        nc.vector.tensor_copy(a_sb[2][:], a_ps[2][:])
+        nc.scalar.copy(a_sb[3][:], a_ps[3][:])
+        nc.vector.tensor_copy(board[2][:].indirect(l3[:]), a_sb[2][:])
+        nc.scalar.activation(board[3][:].indirect(l3[:]), a_sb[3][:], ACT.Copy)
+
+        out_v = out.rearrange("(u p) j -> p u j", p=P)
+        LH = JH // 16
+        seen, diff, hid, hid_w, hid_s, p_ps = [], [], [], [], [], []
+        for h in range(HALVES):
+            seen.append(sb.tile([P, PACK, JH], F32, name=f"seen{h}", align_bytes=64))
+            diff.append(sb.tile([P, PACK, JH], F32, name=f"diff{h}", tag=f"diff{h}", align_bytes=64))
+            hid.append(sb.tile([P, JH * PACK], BF16, name=f"hid{h}", align_bytes=64))
+            hid_w.append(sb.tile([P, JH], U32, name=f"hid_w{h}", align_bytes=64))
+            hid_s.append(sb.tile([P, JH], U8, name=f"hid_s{h}", align_bytes=64))
+            p_ps.append(ps.tile([P, N // P, JH], F32, name=f"p_ps{h}"))
+        for h in range(HALVES):
+            for t in range(PACK):
+                looked = board[t][:].indirect(l4[:, h * LH : (h + 1) * LH])
+                if t % 2 == 0:
+                    nc.vector.tensor_copy(seen[h][:, t, :], looked)
+                else:
+                    nc.scalar.activation(seen[h][:, t, :], looked, ACT.Copy)
+            nc.vector.tensor_tensor(diff[h][:], seen[h][:], b_ps[h][:], ALU.subtract)
+        for h in range(HALVES):
+            nc.scalar.activation(
+                hid[h][:].rearrange("p (c i t) -> p c t i", i=4, t=PACK),
+                diff[h][:].rearrange("p t (c i) -> p c t i", i=4),
+                ACT.Abs,
+            )
+            nc.vector.quantize_mx(out=hid_w[h][:].bitcast(E5M2), scales=hid_s[h][:], in_=hid[h][:])
+            for u in range(N // P):
+                nc.tensor.matmul_mx(
+                    out=p_ps[h][:, u, :], lhsT=wb[:, 2 * P * u : 2 * P * (u + 1)].bitcast(E2M1),
+                    lhsT_scale=wbs[:, P * u : P * (u + 1)],
+                    rhs=hid_w[h][:].bitcast(E5M2), rhs_scale=hid_s[h][:], start=True, stop=True,
+                )
+        for h in range(HALVES):
+            js = slice(h * JH, (h + 1) * JH)
+            tz_seen = sb.tile([P, N // P, JH], F32, name=f"tz_seen{h}", tag=f"diff{h}", align_bytes=64)
+            res = sb.tile([P, N // P, JH], F32, name=f"res{h}", align_bytes=64)
+            for u in range(N // P):
+                looked = tzt[u][:].indirect(l5[:, h * LH : (h + 1) * LH])
+                if h == 0:
+                    nc.vector.tensor_copy(tz_seen[:, u, :], looked)
+                else:
+                    nc.scalar.activation(tz_seen[:, u, :], looked, ACT.Copy)
+            nc.vector.tensor_tensor(res[:], p_ps[h][:], tz_seen[:], ALU.add)
+            nc.sync.dma_start(out=out_v[:, :, js], in_=res[:])

@@ -26,7 +26,7 @@ JH = J // HALVES
 
 def load_rows(queue, plane, scales, q):
     rows = scales[0].bitcast(I32)
-    queue.dma_start(out=plane[QUAD * q : QUAD * q + 4, :].bitcast(I32), in_=rows[4 * q : 4 * q + 4, :])
+    queue.dma_start(out=plane[q:P:QUAD, :].bitcast(I32), in_=rows[q:16:4, :])
 
 
 def load_rows_repeated(queue, plane, scales, q):
@@ -66,7 +66,7 @@ def tile_list_ahead_board_one_tabled_kernel(
 
         nc.vector.memset(xs[:].bitcast(I32), 0)
         for t in range(PACK):
-            nc.vector.memset(board[t][:], 0.0)
+            nc.gpsimd.memset(board[t][:], 0.0)
         nc.sync.dma_start(l1[:], offs)
         load_rows_repeated(nc.sync, ws_raw, w_scales, 0)
         load_rows_repeated(nc.sync, ws_raw, w_scales, 1)
@@ -86,14 +86,14 @@ def tile_list_ahead_board_one_tabled_kernel(
         load_rows_repeated(nc.sync, w2s_raw, w2_scales, 2)
         load_rows_repeated(nc.sync, w2s_raw, w2_scales, 3)
         nc.sync.dma_start(l4[:], offs4)
+        nc.sync.dma_start(l5[:], offs5)
+        nc.sync.dma_start(out=tzt[0][:], in_=tz[0:P, :])
+        nc.sync.dma_start(out=tzt[1][:], in_=tz[P : 2 * P, :])
         nc.sync.dma_start(out=wb[:].bitcast(I32), in_=wb_words[0].bitcast(I32))
         load_rows_repeated(nc.sync, wbs, wb_scales, 0)
         load_rows_repeated(nc.sync, wbs, wb_scales, 1)
         load_rows_repeated(nc.sync, wbs, wb_scales, 2)
         load_rows_repeated(nc.sync, wbs, wb_scales, 3)
-        nc.sync.dma_start(l5[:], offs5)
-        nc.sync.dma_start(out=tzt[0][:], in_=tz[0:P, :])
-        nc.sync.dma_start(out=tzt[1][:], in_=tz[P : 2 * P, :])
 
         def dealt(tile):
             return tile[:].rearrange("p (t m) -> p m t", t=PACK)
@@ -112,7 +112,8 @@ def tile_list_ahead_board_one_tabled_kernel(
 
         nc.vector.tensor_copy(x1s[:], xs[:].indirect(l1[:]))
         nc.vector.tensor_copy(x1w[:], xw[:].indirect(l1[:]))
-        nc.scalar.copy(dealt(w), as_given(w_raw))
+        for i in range(2):
+            nc.scalar.copy(dealt(w)[:, :, 2 * i : 2 * i + 2], as_given(w_raw)[:, :, 2 * i : 2 * i + 2])
         nc.vector.tensor_copy(dealt(ws), as_given(ws_raw))
         nc.scalar.copy(dealt(w2), as_given(w2_raw))
 
@@ -142,7 +143,7 @@ def tile_list_ahead_board_one_tabled_kernel(
         nc.scalar.copy(a_sb[1][:], a_ps[1][:])
         nc.vector.tensor_copy(board[0][:].indirect(l3[:]), a_sb[0][:])
         nc.scalar.activation(board[1][:].indirect(l3[:]), a_sb[1][:], ACT.Copy)
-        nc.vector.tensor_copy(a_sb[2][:], a_ps[2][:])
+        nc.scalar.copy(a_sb[2][:], a_ps[2][:])
         nc.scalar.copy(a_sb[3][:], a_ps[3][:])
         nc.vector.tensor_copy(board[2][:].indirect(l3[:]), a_sb[2][:])
         nc.scalar.activation(board[3][:].indirect(l3[:]), a_sb[3][:], ACT.Copy)
@@ -153,7 +154,7 @@ def tile_list_ahead_board_one_tabled_kernel(
         for h in range(HALVES):
             seen.append(sb.tile([P, PACK, JH], F32, name=f"seen{h}", align_bytes=64))
             diff.append(sb.tile([P, PACK, JH], F32, name=f"diff{h}", tag=f"diff{h}", align_bytes=64))
-            hid.append(sb.tile([P, JH * PACK], BF16, name=f"hid{h}", align_bytes=64))
+            hid.append(sb.tile([P, JH * PACK], BF16, name=f"hid{h}", tag=f"hid{h}", align_bytes=64))
             hid_w.append(sb.tile([P, JH], U32, name=f"hid_w{h}", align_bytes=64))
             hid_s.append(sb.tile([P, JH], U8, name=f"hid_s{h}", align_bytes=64))
             p_ps.append(ps.tile([P, N // P, JH], F32, name=f"p_ps{h}"))
@@ -178,15 +179,11 @@ def tile_list_ahead_board_one_tabled_kernel(
                     lhsT_scale=wbs[:, P * u : P * (u + 1)],
                     rhs=hid_w[h][:].bitcast(E5M2), rhs_scale=hid_s[h][:], start=True, stop=True,
                 )
+        tz_seen = sb.tile([P, N // P, J], F32, name="tz_seen", tag="diff0", align_bytes=64)
+        nc.vector.tensor_copy(tz_seen[:, 0, :], tzt[0][:].indirect(l5[:]))
+        nc.scalar.activation(tz_seen[:, 1, :], tzt[1][:].indirect(l5[:]), ACT.Copy)
         for h in range(HALVES):
             js = slice(h * JH, (h + 1) * JH)
-            tz_seen = sb.tile([P, N // P, JH], F32, name=f"tz_seen{h}", tag=f"diff{h}", align_bytes=64)
-            res = sb.tile([P, N // P, JH], F32, name=f"res{h}", align_bytes=64)
-            for u in range(N // P):
-                looked = tzt[u][:].indirect(l5[:, h * LH : (h + 1) * LH])
-                if h == 0:
-                    nc.vector.tensor_copy(tz_seen[:, u, :], looked)
-                else:
-                    nc.scalar.activation(tz_seen[:, u, :], looked, ACT.Copy)
-            nc.vector.tensor_tensor(res[:], p_ps[h][:], tz_seen[:], ALU.add)
+            res = sb.tile([P, N // P, JH], F32, name=f"res{h}", tag=f"hid{1 - h}", align_bytes=64)
+            nc.vector.tensor_tensor(res[:], p_ps[h][:], tz_seen[:, :, js], ALU.add)
             nc.sync.dma_start(out=out_v[:, :, js], in_=res[:])

@@ -115,7 +115,8 @@ def tile_list_ahead_board_one_tabled_kernel(
         for i in range(2):
             nc.scalar.copy(dealt(w)[:, :, 2 * i : 2 * i + 2], as_given(w_raw)[:, :, 2 * i : 2 * i + 2])
         nc.vector.tensor_copy(dealt(ws), as_given(ws_raw))
-        nc.scalar.copy(dealt(w2), as_given(w2_raw))
+        nc.gpsimd.tensor_copy(dealt(w2), as_given(w2_raw))
+        nc.gpsimd.tensor_copy(dealt(w2s), as_given(w2s_raw))
 
         a_ps = [ps.tile([P, J], F32, name=f"a_ps{t}") for t in range(PACK)]
         for t in range(PACK):
@@ -127,7 +128,6 @@ def tile_list_ahead_board_one_tabled_kernel(
 
         nc.vector.tensor_copy(x2s[:], xs[:].indirect(l2[:]))
         nc.vector.tensor_copy(x2w[:], xw[:].indirect(l2[:]))
-        nc.vector.tensor_copy(dealt(w2s), as_given(w2s_raw))
         b_ps = [ps.tile([P, PACK, JH], F32, name=f"b_ps{h}") for h in range(HALVES)]
         for h in range(HALVES):
             js = slice(h * JH, (h + 1) * JH)

from contextlib import ExitStack

import concourse.mybir as mybir

K, T, J, R, C, N, E = 512, 2048, 256, 512, 512, 256, 1024
FLOPS = 2 * (2 * K * R * J + R * N * J)

F32 = mybir.dt.float32
BF16 = mybir.dt.bfloat16
I32 = mybir.dt.int32
U32 = mybir.dt.uint32
U16 = mybir.dt.uint16
U8 = mybir.dt.uint8
E4M3 = mybir.dt.float8_e4m3fn_x4
E5M2 = mybir.dt.float8_e5m2_x4
E2M1 = mybir.dt.float4_e2m1fn_x4
ALU = mybir.AluOpType
ACT = mybir.ActivationFunctionType

P = 128
PACK = 4
QUAD = 32
HALVES = 2
JH = J // HALVES


def load_rows(queue, plane, scales, q):
    rows = scales[0].bitcast(I32)
    queue.dma_start(out=plane[q:P:QUAD, :].bitcast(I32), in_=rows[q:16:4, :])


def load_rows_repeated(queue, plane, scales, q):
    rows = scales[0].bitcast(I32)
    queue.dma_start(
        out=plane[QUAD * q : QUAD * (q + 1), :].bitcast(I32),
        in_=rows[4 * q : 4 * q + 4, :].partition_broadcast(QUAD // 4),
    )


def tile_list_ahead_board_one_tabled_kernel(
    tc, xt_words, xt_scales, w_words, w_scales, w2_words, w2_scales, wb_words, wb_scales, tz,
    offs, offs2, offs3, offs4, offs5, out,
):
    nc = tc.nc
    with ExitStack() as ctx:
        lists = ctx.enter_context(tc.tile_pool(name="lists", bufs=1))
        sb = ctx.enter_context(tc.tile_pool(name="sb", bufs=1))
        ps = ctx.enter_context(tc.psum_pool(name="ps", bufs=1))

        l1 = lists.tile([P, J // 16], U16, name="l1")
        l2 = lists.tile([P, J // 16], U16, name="l2")
        l3 = lists.tile([P, J // 16], U16, name="l3")
        l4 = lists.tile([P, J // 16], U16, name="l4")
        l5 = lists.tile([P, J // 16], U16, name="l5")

        xw = sb.tile([P, T], U16, name="xw", align_bytes=64)
        xs = sb.tile([P, T], U8, name="xs", align_bytes=64)
        w_raw = sb.tile([P, R], U32, name="w_raw", align_bytes=64)
        ws_raw = sb.tile([P, R], U8, name="ws_raw", align_bytes=64)
        w2_raw = sb.tile([P, R], U32, name="w2_raw", align_bytes=64)
        w2s_raw = sb.tile([P, R], U8, name="w2s_raw", align_bytes=64)
        wb = sb.tile([P, 2 * N], U8, name="wb", align_bytes=64)
        wbs = sb.tile([P, N], U8, name="wbs", align_bytes=64)
        tzt = [sb.tile([P, E], F32, name=f"tz{u}", align_bytes=64) for u in range(N // P)]
        board = [sb.tile([P, C], F32, name=f"board{t}", align_bytes=64) for t in range(PACK)]

        nc.vector.memset(xs[:].bitcast(I32), 0)
        for t in range(PACK):
            nc.gpsimd.memset(board[t][:], 0.0)
        nc.sync.dma_start(l1[:], offs)
        load_rows_repeated(nc.sync, ws_raw, w_scales, 0)
        load_rows_repeated(nc.sync, ws_raw, w_scales, 1)
        load_rows_repeated(nc.sync, ws_raw, w_scales, 2)
        load_rows_repeated(nc.sync, ws_raw, w_scales, 3)
        nc.sync.dma_start(out=xw[:].bitcast(I32), in_=xt_words[0].bitcast(I32))
        load_rows(nc.sync, xs, xt_scales, 0)
        load_rows(nc.sync, xs, xt_scales, 1)
        load_rows(nc.sync, xs, xt_scales, 2)
        load_rows(nc.sync, xs, xt_scales, 3)
        nc.sync.dma_start(out=w_raw[:].bitcast(I32), in_=w_words[0].rearrange("p n t -> p (n t)").bitcast(I32))
        nc.sync.dma_start(l2[:], offs2)
        nc.sync.dma_start(out=w2_raw[:].bitcast(I32), in_=w2_words[0].rearrange("p n t -> p (n t)").bitcast(I32))
        nc.sync.dma_start(l3[:], offs3)
        load_rows_repeated(nc.sync, w2s_raw, w2_scales, 0)
        load_rows_repeated(nc.sync, w2s_raw, w2_scales, 1)
        load_rows_repeated(nc.sync, w2s_raw, w2_scales, 2)
        load_rows_repeated(nc.sync, w2s_raw, w2_scales, 3)
        nc.sync.dma_start(l4[:], offs4)
        nc.sync.dma_start(l5[:], offs5)
        nc.sync.dma_start(out=tzt[0][:], in_=tz[0:P, :])
        nc.sync.dma_start(out=tzt[1][:], in_=tz[P : 2 * P, :])
        nc.sync.dma_start(out=wb[:].bitcast(I32), in_=wb_words[0].bitcast(I32))
        load_rows_repeated(nc.sync, wbs, wb_scales, 0)
        load_rows_repeated(nc.sync, wbs, wb_scales, 1)
        load_rows_repeated(nc.sync, wbs, wb_scales, 2)
        load_rows_repeated(nc.sync, wbs, wb_scales, 3)

        def dealt(tile):
            return tile[:].rearrange("p (t m) -> p m t", t=PACK)

        def as_given(tile):
            return tile[:].rearrange("p (m t) -> p m t", t=PACK)

        x1s = sb.tile([P, J], U8, name="x1s", align_bytes=64)
        x1w = sb.tile([P, J], U16, name="x1w", align_bytes=64)
        x2s = sb.tile([P, J], U8, name="x2s", align_bytes=64)
        x2w = sb.tile([P, J], U16, name="x2w", align_bytes=64)
        w = sb.tile([P, R], U32, name="w", align_bytes=64)
        ws = sb.tile([P, R], U8, name="ws", align_bytes=64)
        w2 = sb.tile([P, R], U32, name="w2", align_bytes=64)
        w2s = sb.tile([P, R], U8, name="w2s", align_bytes=64)

        nc.vector.tensor_copy(x1s[:], xs[:].indirect(l1[:]))
        nc.vector.tensor_copy(x1w[:], xw[:].indirect(l1[:]))
        for i in range(2):
            nc.scalar.copy(dealt(w)[:, :, 2 * i : 2 * i + 2], as_given(w_raw)[:, :, 2 * i : 2 * i + 2])
        nc.vector.tensor_copy(dealt(ws), as_given(ws_raw))
        nc.gpsimd.tensor_copy(dealt(w2), as_given(w2_raw))
        nc.gpsimd.tensor_copy(dealt(w2s), as_given(w2s_raw))

        a_ps = [ps.tile([P, J], F32, name=f"a_ps{t}") for t in range(PACK)]
        for t in range(PACK):
            cols = slice(t * P, (t + 1) * P)
            nc.tensor.matmul_mx(
                out=a_ps[t][:], lhsT=w[:, cols].bitcast(E4M3), lhsT_scale=ws[:, cols],
                rhs=x1w[:].bitcast(E2M1), rhs_scale=x1s[:], start=True, stop=True,
            )

        nc.vector.tensor_copy(x2s[:], xs[:].indirect(l2[:]))
        nc.vector.tensor_copy(x2w[:], xw[:].indirect(l2[:]))
        b_ps = [ps.tile([P, PACK, JH], F32, name=f"b_ps{h}") for h in range(HALVES)]
        for h in range(HALVES):
            js = slice(h * JH, (h + 1) * JH)
            for t in range(PACK):
                cols = slice(t * P, (t + 1) * P)
                nc.tensor.matmul_mx(
                    out=b_ps[h][:, t, :], lhsT=w2[:, cols].bitcast(E5M2), lhsT_scale=w2s[:, cols],
                    rhs=x2w[:, js].bitcast(E2M1), rhs_scale=x2s[:, js], start=True, stop=True,
                )

        a_sb = [sb.tile([P, J], F32, name=f"a_sb{t}", align_bytes=64) for t in range(PACK)]
        nc.scalar.copy(a_sb[0][:], a_ps[0][:])
        nc.scalar.copy(a_sb[1][:], a_ps[1][:])
        nc.vector.tensor_copy(board[0][:].indirect(l3[:]), a_sb[0][:])
        nc.scalar.activation(board[1][:].indirect(l3[:]), a_sb[1][:], ACT.Copy)
        nc.scalar.copy(a_sb[2][:], a_ps[2][:])
        nc.scalar.copy(a_sb[3][:], a_ps[3][:])
        nc.vector.tensor_copy(board[2][:].indirect(l3[:]), a_sb[2][:])
        nc.scalar.activation(board[3][:].indirect(l3[:]), a_sb[3][:], ACT.Copy)

        out_v = out.rearrange("(u p) j -> p u j", p=P)
        LH = JH // 16
        seen, diff, hid, hid_w, hid_s, p_ps = [], [], [], [], [], []
        for h in range(HALVES):
            seen.append(sb.tile([P, PACK, JH], F32, name=f"seen{h}", align_bytes=64))
            diff.append(sb.tile([P, PACK, JH], F32, name=f"diff{h}", tag=f"diff{h}", align_bytes=64))
            hid.append(sb.tile([P, JH * PACK], BF16, name=f"hid{h}", tag=f"hid{h}", align_bytes=64))
            hid_w.append(sb.tile([P, JH], U32, name=f"hid_w{h}", align_bytes=64))
            hid_s.append(sb.tile([P, JH], U8, name=f"hid_s{h}", align_bytes=64))
            p_ps.append(ps.tile([P, N // P, JH], F32, name=f"p_ps{h}"))
        for h in range(HALVES):
            for t in range(PACK):
                looked = board[t][:].indirect(l4[:, h * LH : (h + 1) * LH])
                if t % 2 == 0:
                    nc.vector.tensor_copy(seen[h][:, t, :], looked)
                else:
                    nc.scalar.activation(seen[h][:, t, :], looked, ACT.Copy)
            nc.vector.tensor_tensor(diff[h][:], seen[h][:], b_ps[h][:], ALU.subtract)
        for h in range(HALVES):
            nc.scalar.activation(
                hid[h][:].rearrange("p (c i t) -> p c t i", i=4, t=PACK),
                diff[h][:].rearrange("p t (c i) -> p c t i", i=4),
                ACT.Abs,
            )
            nc.vector.quantize_mx(out=hid_w[h][:].bitcast(E5M2), scales=hid_s[h][:], in_=hid[h][:])
            for u in range(N // P):
                nc.tensor.matmul_mx(
                    out=p_ps[h][:, u, :], lhsT=wb[:, 2 * P * u : 2 * P * (u + 1)].bitcast(E2M1),
                    lhsT_scale=wbs[:, P * u : P * (u + 1)],
                    rhs=hid_w[h][:].bitcast(E5M2), rhs_scale=hid_s[h][:], start=True, stop=True,
                )
        tz_seen = sb.tile([P, N // P, J], F32, name="tz_seen", tag="diff0", align_bytes=64)
        nc.vector.tensor_copy(tz_seen[:, 0, :], tzt[0][:].indirect(l5[:]))
        nc.scalar.activation(tz_seen[:, 1, :], tzt[1][:].indirect(l5[:]), ACT.Copy)
        for h in range(HALVES):
            js = slice(h * JH, (h + 1) * JH)
            res = sb.tile([P, N // P, JH], F32, name=f"res{h}", tag=f"hid{1 - h}", align_bytes=64)
            nc.vector.tensor_tensor(res[:], p_ps[h][:], tz_seen[:, :, js], ALU.add)
            nc.sync.dma_start(out=out_v[:, :, js], in_=res[:])
